import numpy as np
import ml_dtypes


def mxq(x, axis, fmt="e4m3"):
    dtype, down = {"e4m3": (ml_dtypes.float8_e4m3fn, 7), "e5m2": (ml_dtypes.float8_e5m2, 14)}[fmt]
    v = np.moveaxis(np.asarray(x, np.float32).astype(ml_dtypes.bfloat16).astype(np.float64), axis, -1)
    blocks = v.reshape(v.shape[:-1] + (-1, 32))
    amax = np.abs(blocks).max(-1, keepdims=True)
    byte = np.maximum(np.where(amax > 0, np.frexp(amax)[1] - 1 + 127, 0) - down, 1)
    scale = np.exp2(byte - 127.0)
    codes = (blocks / scale).astype(np.float32).astype(dtype).astype(np.float64)
    return np.moveaxis((codes * scale).reshape(v.shape), -1, axis)


WIDE = False


def mx_kscale(k):
    if not WIDE:
        return np.ones(k)
    levels = np.array([10, -10, 5, -5, 0])
    if k % 512:
        return np.exp2(np.random.permutation(np.resize(levels, k // 32))).repeat(32)
    a = np.empty((k // 512, 16))
    for p in range(k // 512):
        a[p, :8] = np.random.permutation(np.resize(levels, 8))
        for g in range(8):
            far = levels[np.abs(levels - a[p, g]) >= 10]
            a[p, g + 8] = far[np.random.randint(len(far))]
    return np.exp2(a.ravel()).repeat(32)


def f64(x):
    return np.asarray(x).astype(np.float64)


def striped(idx):
    return np.tile(np.asarray(idx).reshape(-1, 16).T, (8, 1)).astype(np.uint16)


def unstriped(offs):
    return offs[:16].T.reshape(-1).astype(np.int64)


E2M1 = np.array([0.0, 0.5, 1.0, 1.5, 2.0, 3.0, 4.0, 6.0, -0.0, -0.5, -1.0, -1.5, -2.0, -3.0, -4.0, -6.0])


def pack_weight(w, fmt):
    k, n = w.shape
    w = f64(np.asarray(w, np.float32).astype(ml_dtypes.bfloat16)).reshape(k // 32, 32, n)
    amax = np.abs(w).max(1)
    if fmt == "e4m3":
        byte = np.frexp(amax)[1] - 1 + 127 - 7
    else:
        mant, ex = np.frexp(amax / 6.0)
        byte = np.where(mant > 0.5, ex, ex - 1) + 127
    byte = np.clip(np.where(amax > 0, byte, 1), 1, 254)
    scaled = (w * np.exp2(127.0 - byte)[:, None, :]).reshape(k, n).astype(np.float32)
    by_word = np.ascontiguousarray(scaled.reshape(k // 512, 128, 4, n).transpose(0, 1, 3, 2))
    if fmt == "e4m3":
        words = by_word.astype(ml_dtypes.float8_e4m3fn).view(np.uint8)
    else:
        c = by_word.astype(ml_dtypes.float4_e2m1fn).view(np.uint8) & 0xF
        words = (c[..., 0::2] | (c[..., 1::2] << 4)).reshape(k // 512, 128, 2 * n)
    return np.ascontiguousarray(words), np.ascontiguousarray(byte.astype(np.uint8).reshape(k // 512, 16, n))


def unpack_weight(words, scales, fmt):
    g, _, n = scales.shape
    words = np.ascontiguousarray(words).reshape(g, 128, n, -1)
    if fmt == "e4m3":
        vals = words.view(ml_dtypes.float8_e4m3fn).astype(np.float64)
    else:
        nib = np.empty((g, 128, n, 4), np.uint8)
        nib[..., 0::2] = words & 0xF
        nib[..., 1::2] = words >> 4
        vals = E2M1[nib]
    vals = vals * np.repeat(np.exp2(scales.astype(np.float64) - 127.0), 8, axis=1)[..., None]
    return vals.transpose(0, 1, 3, 2).reshape(g * 512, n)


K, T, N, J = 512, 512, 2048, 512


def setup_inputs():
    n = np.random.standard_normal
    idx = np.random.permutation(N)[:J]
    fk = mx_kscale(K)
    xqp = pack_weight(n((K, T)) * 0.8 / fk[:, None], "e2m1")
    wbp = pack_weight(n((K, N)) * 1 / np.sqrt(K) * fk[:, None], "e2m1")
    wop = pack_weight(n((K, J)) * 1 / np.sqrt(K) * fk[:, None], "e4m3")
    return {
        "xq_words": xqp[0],
        "xq_scales": xqp[1],
        "wb_words": wbp[0],
        "wb_scales": wbp[1],
        "xf": (n((K, T)) / fk[:, None]).astype(np.float32),
        "wo_words": wop[0],
        "wo_scales": wop[1],
        "b": (np.random.uniform(-0.5, 0.5, (1, N))).astype(np.float32),
        "offs": striped(idx),
    }


def reference(xq_words, xq_scales, wb_words, wb_scales, xf, wo_words, wo_scales, b, offs):
    idx = unstriped(offs)
    xqu = unpack_weight(xq_words, xq_scales, "e2m1")
    wbu = unpack_weight(wb_words, wb_scales, "e2m1")
    wou = unpack_weight(wo_words, wo_scales, "e4m3")
    z = xqu.T @ wbu
    xfq = mxq(f64(xf), 0, "e4m3")
    p = xfq.T @ wou
    pg = np.zeros((T, N))
    pg[:, idx] = p
    y = z + pg + f64(b)
    return y

@@ -1,0 +1,182 @@
+from contextlib import ExitStack
+
+import concourse.mybir as mybir
+from concourse.masks import make_identity
+
+K, T, N, J = 512, 512, 2048, 512
+FLOPS = 2 * K * T * N + 2 * K * T * J
+
+F32 = mybir.dt.float32
+BF16 = mybir.dt.bfloat16
+I32 = mybir.dt.int32
+U32 = mybir.dt.uint32
+U16 = mybir.dt.uint16
+U8 = mybir.dt.uint8
+FP8X4 = mybir.dt.float8_e4m3fn_x4
+FP4X4 = mybir.dt.float4_e2m1fn_x4
+ADD = mybir.AluOpType.add
+IDENT = mybir.ActivationFunctionType.Identity
+
+P = 128
+PACK = 4
+BANK = 512
+TILES = T // P
+CHUNKS = N // BANK
+BLOCKS = BANK // P
+
+
+def load_scales(nc, plane, scales):
+    rows = scales[0].bitcast(I32).rearrange("(q r) n -> r q n", r=4)
+    words = plane[:].bitcast(I32)
+    for r in range(4):
+        nc.sync.dma_start(out=words[r:P:32, :], in_=rows[r])
+
+
+def interleave(nc, grouped, raw):
+    nc.vector.tensor_copy(
+        out=grouped.rearrange("p (c i j) -> p c j i", i=4, j=PACK),
+        in_=raw.rearrange("p j (c i) -> p c j i", i=4),
+    )
+
+
+def tile_list_outlier_features_out_kernel(tc, xq_words, xq_scales, wb_words, wb_scales, xf, wo_words, wo_scales, b, offs, out):
+    nc = tc.nc
+    with ExitStack() as ctx:
+        keep = ctx.enter_context(tc.tile_pool(name="keep", bufs=1))
+        late = ctx.enter_context(tc.tile_pool(name="late", bufs=1))
+        psum = ctx.enter_context(tc.psum_pool(name="psum", bufs=1))
+
+        offsets = keep.tile([P, J // 16], U16, name="offsets")
+        ident = keep.tile([P, P], F32, name="ident")
+        wo_plane = keep.tile([P, J], U8, name="wo_plane", align_bytes=64)
+        xq_plane = keep.tile([P, T], U8, name="xq_plane", align_bytes=64)
+        wb_plane = keep.tile([P, N], U8, name="wb_plane", align_bytes=64)
+        wo_codes = keep.tile([P, J], U32, name="wo_codes", align_bytes=64)
+        xq_codes = keep.tile([P, 2 * T], U8, name="xq_codes", align_bytes=64)
+        wb_codes = keep.tile([P, 2 * N], U8, name="wb_codes", align_bytes=64)
+        raw_a = keep.tile([P, PACK, 2 * P], F32, name="raw_a")
+        raw_b = keep.tile([P, PACK, 2 * P], F32, name="raw_b")
+        g0 = keep.tile([P, PACK * P], BF16, name="g0", align_bytes=64)
+        g1 = keep.tile([P, PACK * P], BF16, name="g1", align_bytes=64)
+        g23 = late.tile([P, 2 * PACK * P], BF16, name="g23", align_bytes=64, offset=4 * N - 1024)
+        xf_codes = keep.tile([P, T], U32, name="xf_codes", align_bytes=64)
+        xf_plane = keep.tile([P, T], U8, name="xf_plane", align_bytes=64)
+        b_rows = keep.tile([P, P], F32, name="b_rows")
+        b_cols = keep.tile([P, N // P], F32, name="b_cols")
+        banks = [psum.tile([P, BANK], F32, name=f"bank{k}") for k in range(8)]
+
+        nc.gpsimd.memset(wo_plane[:].bitcast(U32), 0)
+        nc.gpsimd.memset(xq_plane[:].bitcast(U32), 0)
+        nc.gpsimd.memset(wb_plane[:].bitcast(U32), 0)
+        make_identity(nc, ident[:])
+        nc.scalar.activation(out=b_rows[:], in_=ident[:], func=IDENT, scale=0.0)
+
+        xf_rows = xf.rearrange("(p j) t -> p j t", j=PACK)
+        nc.sync.dma_start(out=raw_a[:], in_=xf_rows[:, :, 0 : 2 * P])
+        nc.sync.dma_start(out=wo_codes[:].bitcast(I32), in_=wo_words[0].rearrange("p n t -> p (n t)").bitcast(I32))
+        load_scales(nc, wo_plane, wo_scales)
+        nc.sync.dma_start(out=raw_b[:], in_=xf_rows[:, :, 2 * P : T])
+        nc.sync.dma_start(offsets[:], offs)
+        nc.sync.dma_start(out=xq_codes[:].bitcast(I32), in_=xq_words[0].bitcast(I32))
+        nc.sync.dma_start(out=wb_codes[:].bitcast(I32), in_=wb_words[0].bitcast(I32))
+        nc.sync.dma_start(out=b_rows[0 : N // P, :], in_=b.rearrange("o (c m) -> (o c) m", m=P))
+        load_scales(nc, xq_plane, xq_scales)
+        load_scales(nc, wb_plane, wb_scales)
+
+        pages = [keep.tile([P, N], F32, name="page0")]
+        nc.vector.memset(pages[0][:], 0.0)
+
+        def quantize(grouped, t0, t1):
+            nc.vector.quantize_mx(out=xf_codes[:, t0:t1].bitcast(FP8X4), scales=xf_plane[:, t0:t1], in_=grouped)
+
+        interleave(nc, g0[:], raw_a[:, :, 0:P])
+        interleave(nc, g1[:], raw_a[:, :, P : 2 * P])
+        quantize(g0[:], 0, P)
+        quantize(g1[:], P, 2 * P)
+        interleave(nc, g23[:], raw_b[:])
+        quantize(g23[:], 2 * P, T)
+
+        def clear_page(i):
+            page = late.tile([P, N], F32, name=f"page{i}", offset=4 * N * (i - 1))
+            nc.gpsimd.memset(page[:], 0.0)
+            pages.append(page)
+
+        clear_page(1)
+        clear_page(2)
+
+        p_tiles = []
+        for i in range(TILES):
+            tok = slice(i * P, (i + 1) * P)
+            acc = banks[3 + i % 2]
+            nc.tensor.matmul_mx(out=acc[:], lhsT=xf_codes[:, tok].bitcast(FP8X4), lhsT_scale=xf_plane[:, tok],
+                                rhs=wo_codes[:].bitcast(FP8X4), rhs_scale=wo_plane[:], start=True, stop=True)
+            p_sb = keep.tile([P, J], F32, name=f"p{i}")
+            nc.scalar.copy(out=p_sb[:], in_=acc[:])
+            p_tiles.append(p_sb)
+
+        def scatter(i):
+            nc.vector.tensor_copy(pages[i][:].indirect(offsets[:]), p_tiles[i][:])
+
+        for i in range(3):
+            scatter(i)
+
+        nc.tensor.transpose(banks[5][:, 0:P], b_rows[:], ident[:])
+        nc.scalar.copy(out=b_cols[:], in_=banks[5][:, 0 : N // P])
+
+        zb = []
+
+        def products(c):
+            for j in range(BLOCKS):
+                nb = c * BLOCKS + j
+                acc = banks[nb % 3]
+                nc.tensor.matmul_mx(out=acc[:], lhsT=wb_codes[:, 2 * P * nb : 2 * P * (nb + 1)].bitcast(FP4X4),
+                                    lhsT_scale=wb_plane[:, P * nb : P * (nb + 1)],
+                                    rhs=xq_codes[:].bitcast(FP4X4), rhs_scale=xq_plane[:], start=True, stop=True)
+                z_sb = keep.tile([P, T], F32, name=f"zb{nb}")
+                nc.scalar.activation(out=z_sb[:], in_=acc[:], func=IDENT, bias=b_cols[:, nb : nb + 1])
+                zb.append(z_sb)
+
+        def turn(i, c, acc):
+            for j in range(BLOCKS):
+                nc.tensor.transpose(acc[:, j * P : (j + 1) * P], zb[c * BLOCKS + j][:, i * P : (i + 1) * P], ident[:])
+
+        def store(i, c, res):
+            nc.sync.dma_start(out=out[i * P : (i + 1) * P, c * BANK : (c + 1) * BANK], in_=res[:])
+
+        def g_unit(i, c, stage):
+            turn(i, c, banks[3 + i])
+            nc.scalar.copy(out=stage[:], in_=banks[3 + i][:])
+            res = keep.tile([P, BANK], F32, name=f"res{i}_{c}")
+            nc.gpsimd.tensor_tensor(res[:], stage[:], pages[i][:, c * BANK : (c + 1) * BANK], ADD)
+            store(i, c, res)
+
+        def v_unit(i, c, k, res):
+            turn(i, c, banks[k])
+            nc.vector.tensor_tensor(res[:], banks[k][:], pages[i][:, c * BANK : (c + 1) * BANK], ADD)
+            store(i, c, res)
+
+        def fresh(name):
+            return keep.tile([P, BANK], F32, name=name)
+
+        products(0)
+        g_unit(0, 0, late.tile([P, BANK], F32, name="stage00", offset=4 * N * 2))
+        clear_page(3)
+        g_unit(1, 0, fresh("stage10"))
+        v_unit(2, 0, 5, fresh("res20"))
+        products(1)
+        g_unit(0, 1, fresh("stage01"))
+        g_unit(1, 1, fresh("stage11"))
+        v_unit(2, 1, 7, fresh("res21"))
+        scatter(3)
+        products(2)
+        g_unit(0, 2, fresh("stage02"))
+        g_unit(1, 2, late.tile([P, BANK], F32, name="stage12", offset=4 * N * 3))
+        v_unit(3, 0, 6, late.tile([P, BANK], F32, name="res30", offset=4 * N * 3))
+        products(3)
+        g_unit(0, 3, fresh("stage03"))
+        g_unit(1, 3, fresh("stage13"))
+        v_unit(3, 1, 1, fresh("res31"))
+        v_unit(2, 2, 2, fresh("res22"))
+        v_unit(3, 2, 0, fresh("res32"))
+        v_unit(2, 3, 5, fresh("res23"))
+        v_unit(3, 3, 7, fresh("res33"))

@@ -25,11 +25,11 @@ CHUNKS = N // BANK
 BLOCKS = BANK // P
 
 
-def load_scales(nc, plane, scales):
+def load_scales(queues, plane, scales):
     rows = scales[0].bitcast(I32).rearrange("(q r) n -> r q n", r=4)
     words = plane[:].bitcast(I32)
     for r in range(4):
-        nc.sync.dma_start(out=words[r:P:32, :], in_=rows[r])
+        queues[r].dma_start(out=words[r:P:32, :], in_=rows[r])
 
 
 def interleave(nc, grouped, raw):
@@ -67,24 +67,24 @@ def tile_list_outlier_features_out_kernel(tc, xq_words, xq_scales, wb_words, wb_
 
         nc.gpsimd.memset(wo_plane[:].bitcast(U32), 0)
         nc.gpsimd.memset(xq_plane[:].bitcast(U32), 0)
-        nc.gpsimd.memset(wb_plane[:].bitcast(U32), 0)
-        make_identity(nc, ident[:])
-        nc.scalar.activation(out=b_rows[:], in_=ident[:], func=IDENT, scale=0.0)
+        nc.gpsimd.memset(b_rows[:], 0.0)
+        nc.vector.memset(wb_plane[:].bitcast(U32), 0)
 
         xf_rows = xf.rearrange("(p j) t -> p j t", j=PACK)
         nc.sync.dma_start(out=raw_a[:], in_=xf_rows[:, :, 0 : 2 * P])
         nc.sync.dma_start(out=wo_codes[:].bitcast(I32), in_=wo_words[0].rearrange("p n t -> p (n t)").bitcast(I32))
-        load_scales(nc, wo_plane, wo_scales)
+        load_scales([nc.sync] * 4, wo_plane, wo_scales)
         nc.sync.dma_start(out=raw_b[:], in_=xf_rows[:, :, 2 * P : T])
         nc.sync.dma_start(offsets[:], offs)
         nc.sync.dma_start(out=xq_codes[:].bitcast(I32), in_=xq_words[0].bitcast(I32))
         nc.sync.dma_start(out=wb_codes[:].bitcast(I32), in_=wb_words[0].bitcast(I32))
-        nc.sync.dma_start(out=b_rows[0 : N // P, :], in_=b.rearrange("o (c m) -> (o c) m", m=P))
-        load_scales(nc, xq_plane, xq_scales)
-        load_scales(nc, wb_plane, wb_scales)
+        load_scales([nc.gpsimd, nc.gpsimd, nc.sync, nc.sync], xq_plane, xq_scales)
+        nc.gpsimd.dma_start(out=b_rows[0 : N // P, :], in_=b.rearrange("o (c m) -> (o c) m", m=P))
+        make_identity(nc, ident[:])
+        load_scales([nc.sync] * 4, wb_plane, wb_scales)
 
         pages = [keep.tile([P, N], F32, name="page0")]
-        nc.vector.memset(pages[0][:], 0.0)
+        nc.vector.memset(pages[0][:].bitcast(U32), 0)
 
         def quantize(grouped, t0, t1):
             nc.vector.quantize_mx(out=xf_codes[:, t0:t1].bitcast(FP8X4), scales=xf_plane[:, t0:t1], in_=grouped)
@@ -110,14 +110,16 @@ def tile_list_outlier_features_out_kernel(tc, xq_words, xq_scales, wb_words, wb_
             acc = banks[3 + i % 2]
             nc.tensor.matmul_mx(out=acc[:], lhsT=xf_codes[:, tok].bitcast(FP8X4), lhsT_scale=xf_plane[:, tok],
                                 rhs=wo_codes[:].bitcast(FP8X4), rhs_scale=wo_plane[:], start=True, stop=True)
-            p_sb = keep.tile([P, J], F32, name=f"p{i}")
+            p_sb = late.tile([P, J], F32, name=f"p{i}", offset=4 * N * 2 if i == 0 else 4 * N * 3 + 4 * J * i)
             nc.scalar.copy(out=p_sb[:], in_=acc[:])
             p_tiles.append(p_sb)
 
         def scatter(i):
             nc.vector.tensor_copy(pages[i][:].indirect(offsets[:]), p_tiles[i][:])
 
-        for i in range(3):
+        scatter(0)
+        clear_page(3)
+        for i in range(1, TILES):
             scatter(i)
 
         nc.tensor.transpose(banks[5][:, 0:P], b_rows[:], ident[:])
@@ -125,10 +127,10 @@ def tile_list_outlier_features_out_kernel(tc, xq_words, xq_scales, wb_words, wb_
 
         zb = []
 
-        def products(c):
-            for j in range(BLOCKS):
-                nb = c * BLOCKS + j
-                acc = banks[nb % 3]
+        def products(ks):
+            for k in ks:
+                nb = len(zb)
+                acc = banks[k]
                 nc.tensor.matmul_mx(out=acc[:], lhsT=wb_codes[:, 2 * P * nb : 2 * P * (nb + 1)].bitcast(FP4X4),
                                     lhsT_scale=wb_plane[:, P * nb : P * (nb + 1)],
                                     rhs=xq_codes[:].bitcast(FP4X4), rhs_scale=xq_plane[:], start=True, stop=True)
@@ -143,40 +145,37 @@ def tile_list_outlier_features_out_kernel(tc, xq_words, xq_scales, wb_words, wb_
         def store(i, c, res):
             nc.sync.dma_start(out=out[i * P : (i + 1) * P, c * BANK : (c + 1) * BANK], in_=res[:])
 
-        def g_unit(i, c, stage):
-            turn(i, c, banks[3 + i])
-            nc.scalar.copy(out=stage[:], in_=banks[3 + i][:])
+        def g_unit(i, c, k):
+            turn(i, c, banks[k])
+            stage = keep.tile([P, BANK], F32, name=f"stage{i}_{c}")
+            nc.scalar.copy(out=stage[:], in_=banks[k][:])
             res = keep.tile([P, BANK], F32, name=f"res{i}_{c}")
             nc.gpsimd.tensor_tensor(res[:], stage[:], pages[i][:, c * BANK : (c + 1) * BANK], ADD)
             store(i, c, res)
 
-        def v_unit(i, c, k, res):
+        def v_unit(i, c, k):
             turn(i, c, banks[k])
+            res = keep.tile([P, BANK], F32, name=f"res{i}_{c}")
             nc.vector.tensor_tensor(res[:], banks[k][:], pages[i][:, c * BANK : (c + 1) * BANK], ADD)
             store(i, c, res)
 
-        def fresh(name):
-            return keep.tile([P, BANK], F32, name=name)
-
-        products(0)
-        g_unit(0, 0, late.tile([P, BANK], F32, name="stage00", offset=4 * N * 2))
-        clear_page(3)
-        g_unit(1, 0, fresh("stage10"))
-        v_unit(2, 0, 5, fresh("res20"))
-        products(1)
-        g_unit(0, 1, fresh("stage01"))
-        g_unit(1, 1, fresh("stage11"))
-        v_unit(2, 1, 7, fresh("res21"))
-        scatter(3)
-        products(2)
-        g_unit(0, 2, fresh("stage02"))
-        g_unit(1, 2, late.tile([P, BANK], F32, name="stage12", offset=4 * N * 3))
-        v_unit(3, 0, 6, late.tile([P, BANK], F32, name="res30", offset=4 * N * 3))
-        products(3)
-        g_unit(0, 3, fresh("stage03"))
-        g_unit(1, 3, fresh("stage13"))
-        v_unit(3, 1, 1, fresh("res31"))
-        v_unit(2, 2, 2, fresh("res22"))
-        v_unit(3, 2, 0, fresh("res32"))
-        v_unit(2, 3, 5, fresh("res23"))
-        v_unit(3, 3, 7, fresh("res33"))
+        products([0, 1, 2, 0])
+        g_unit(0, 0, 3)
+        g_unit(1, 0, 4)
+        products([1, 2, 0, 1])
+        g_unit(0, 1, 3)
+        g_unit(1, 1, 4)
+        products([2, 5, 6, 7, 0, 1])
+        g_unit(0, 2, 3)
+        g_unit(1, 2, 4)
+        v_unit(2, 0, 5)
+        v_unit(3, 0, 6)
+        v_unit(2, 1, 7)
+        v_unit(3, 1, 0)
+        v_unit(2, 2, 1)
+        products([2, 3])
+        g_unit(0, 3, 4)
+        v_unit(3, 2, 2)
+        v_unit(1, 3, 5)
+        v_unit(2, 3, 6)
+        v_unit(3, 3, 7)

@@ -15,89 +15,98 @@ U8 = mybir.dt.uint8
 FP8X4 = mybir.dt.float8_e4m3fn_x4
 FP4X4 = mybir.dt.float4_e2m1fn_x4
 ADD = mybir.AluOpType.add
-IDENT = mybir.ActivationFunctionType.Identity
+IDENTITY = mybir.ActivationFunctionType.Identity
 
 P = 128
 PACK = 4
-BANK = 512
+CHUNK = 512
 TILES = T // P
-CHUNKS = N // BANK
-BLOCKS = BANK // P
+CHUNKS = N // CHUNK
+BLOCKS = CHUNK // P
+PAGE_BYTES = 4 * N
+RUN = 4
+
+STAGE_BANKS = (4, 5)
+SPARE_BANKS = (6, 7)
 
 
-def load_scales(queues, plane, scales):
+def load_scales(queues, scale_tile, scales):
     rows = scales[0].bitcast(I32).rearrange("(q r) n -> r q n", r=4)
-    words = plane[:].bitcast(I32)
+    dst = scale_tile[:].bitcast(I32)
     for r in range(4):
-        queues[r].dma_start(out=words[r:P:32, :], in_=rows[r])
+        queues[r].dma_start(out=dst[r:P:32, :], in_=rows[r])
 
 
 def interleave(nc, grouped, raw):
     nc.vector.tensor_copy(
-        out=grouped.rearrange("p (c i j) -> p c j i", i=4, j=PACK),
-        in_=raw.rearrange("p j (c i) -> p c j i", i=4),
+        out=grouped.rearrange("p (c i j) -> p c j i", i=RUN, j=PACK),
+        in_=raw.rearrange("p j (c i) -> p c j i", i=RUN),
     )
 
 
-def tile_list_outlier_features_out_kernel(tc, xq_words, xq_scales, wb_words, wb_scales, xf, wo_words, wo_scales, b, offs, out):
+def tile_list_outlier_features_out_kernel(
+    tc, xq_words, xq_scales, wb_words, wb_scales, xf, wo_words, wo_scales, b, offs, out
+):
     nc = tc.nc
     with ExitStack() as ctx:
         keep = ctx.enter_context(tc.tile_pool(name="keep", bufs=1))
-        late = ctx.enter_context(tc.tile_pool(name="late", bufs=1))
+        shared = ctx.enter_context(tc.tile_pool(name="shared", bufs=1))
         psum = ctx.enter_context(tc.psum_pool(name="psum", bufs=1))
 
         offsets = keep.tile([P, J // 16], U16, name="offsets")
         ident = keep.tile([P, P], F32, name="ident")
-        wo_plane = keep.tile([P, J], U8, name="wo_plane", align_bytes=64)
-        xq_plane = keep.tile([P, T], U8, name="xq_plane", align_bytes=64)
-        wb_plane = keep.tile([P, N], U8, name="wb_plane", align_bytes=64)
+        wo_scale = keep.tile([P, J], U8, name="wo_scale", align_bytes=64)
+        xq_scale = keep.tile([P, T], U8, name="xq_scale", align_bytes=64)
+        wb_scale = keep.tile([P, N], U8, name="wb_scale", align_bytes=64)
         wo_codes = keep.tile([P, J], U32, name="wo_codes", align_bytes=64)
         xq_codes = keep.tile([P, 2 * T], U8, name="xq_codes", align_bytes=64)
         wb_codes = keep.tile([P, 2 * N], U8, name="wb_codes", align_bytes=64)
-        raw_a = keep.tile([P, PACK, 2 * P], F32, name="raw_a")
-        raw_b = keep.tile([P, PACK, 2 * P], F32, name="raw_b")
-        g0 = keep.tile([P, PACK * P], BF16, name="g0", align_bytes=64)
-        g1 = keep.tile([P, PACK * P], BF16, name="g1", align_bytes=64)
-        g23 = late.tile([P, 2 * PACK * P], BF16, name="g23", align_bytes=64, offset=4 * N - 1024)
+        xf_low = keep.tile([P, PACK, 2 * P], F32, name="xf_low")
+        xf_high = keep.tile([P, PACK, 2 * P], F32, name="xf_high")
+        grouped0 = keep.tile([P, PACK * P], BF16, name="grouped0", align_bytes=64)
+        grouped1 = keep.tile([P, PACK * P], BF16, name="grouped1", align_bytes=64)
+        grouped23 = shared.tile([P, 2 * PACK * P], BF16, name="grouped23", align_bytes=64, offset=PAGE_BYTES - 1024)
         xf_codes = keep.tile([P, T], U32, name="xf_codes", align_bytes=64)
-        xf_plane = keep.tile([P, T], U8, name="xf_plane", align_bytes=64)
+        xf_scale = keep.tile([P, T], U8, name="xf_scale", align_bytes=64)
         b_rows = keep.tile([P, P], F32, name="b_rows")
         b_cols = keep.tile([P, N // P], F32, name="b_cols")
-        banks = [psum.tile([P, BANK], F32, name=f"bank{k}") for k in range(8)]
+        banks = [psum.tile([P, CHUNK], F32, name=f"bank{k}") for k in range(8)]
 
-        nc.gpsimd.memset(wo_plane[:].bitcast(U32), 0)
-        nc.gpsimd.memset(xq_plane[:].bitcast(U32), 0)
+        nc.gpsimd.memset(wo_scale[:].bitcast(U32), 0)
+        nc.gpsimd.memset(xq_scale[:].bitcast(U32), 0)
         nc.gpsimd.memset(b_rows[:], 0.0)
-        nc.vector.memset(wb_plane[:].bitcast(U32), 0)
+        nc.vector.memset(wb_scale[:].bitcast(U32), 0)
 
         xf_rows = xf.rearrange("(p j) t -> p j t", j=PACK)
-        nc.sync.dma_start(out=raw_a[:], in_=xf_rows[:, :, 0 : 2 * P])
-        nc.sync.dma_start(out=wo_codes[:].bitcast(I32), in_=wo_words[0].rearrange("p n t -> p (n t)").bitcast(I32))
-        load_scales([nc.sync] * 4, wo_plane, wo_scales)
-        nc.sync.dma_start(out=raw_b[:], in_=xf_rows[:, :, 2 * P : T])
         nc.sync.dma_start(offsets[:], offs)
-        nc.sync.dma_start(out=xq_codes[:].bitcast(I32), in_=xq_words[0].bitcast(I32))
+        nc.sync.dma_start(out=xf_low[:], in_=xf_rows[:, :, 0 : 2 * P])
+        nc.sync.dma_start(out=wo_codes[:].bitcast(I32), in_=wo_words[0].rearrange("p n t -> p (n t)").bitcast(I32))
+        load_scales([nc.sync] * 4, wo_scale, wo_scales)
+        nc.sync.dma_start(out=xf_high[:], in_=xf_rows[:, :, 2 * P : T])
         nc.sync.dma_start(out=wb_codes[:].bitcast(I32), in_=wb_words[0].bitcast(I32))
-        load_scales([nc.gpsimd, nc.gpsimd, nc.sync, nc.sync], xq_plane, xq_scales)
+        nc.sync.dma_start(out=xq_codes[:].bitcast(I32), in_=xq_words[0].bitcast(I32))
+        load_scales([nc.gpsimd, nc.gpsimd, nc.sync, nc.sync], xq_scale, xq_scales)
         nc.gpsimd.dma_start(out=b_rows[0 : N // P, :], in_=b.rearrange("o (c m) -> (o c) m", m=P))
         make_identity(nc, ident[:])
-        load_scales([nc.sync] * 4, wb_plane, wb_scales)
+        load_scales([nc.sync] * 4, wb_scale, wb_scales)
 
         pages = [keep.tile([P, N], F32, name="page0")]
         nc.vector.memset(pages[0][:].bitcast(U32), 0)
 
-        def quantize(grouped, t0, t1):
-            nc.vector.quantize_mx(out=xf_codes[:, t0:t1].bitcast(FP8X4), scales=xf_plane[:, t0:t1], in_=grouped)
+        def quantize(grouped, first, last):
+            nc.vector.quantize_mx(
+                out=xf_codes[:, first:last].bitcast(FP8X4), scales=xf_scale[:, first:last], in_=grouped[:]
+            )
 
-        interleave(nc, g0[:], raw_a[:, :, 0:P])
-        interleave(nc, g1[:], raw_a[:, :, P : 2 * P])
-        quantize(g0[:], 0, P)
-        quantize(g1[:], P, 2 * P)
-        interleave(nc, g23[:], raw_b[:])
-        quantize(g23[:], 2 * P, T)
+        interleave(nc, grouped0[:], xf_low[:, :, 0:P])
+        interleave(nc, grouped1[:], xf_low[:, :, P : 2 * P])
+        quantize(grouped0, 0, P)
+        quantize(grouped1, P, 2 * P)
+        interleave(nc, grouped23[:], xf_high[:])
+        quantize(grouped23, 2 * P, T)
 
         def clear_page(i):
-            page = late.tile([P, N], F32, name=f"page{i}", offset=4 * N * (i - 1))
+            page = shared.tile([P, N], F32, name=f"page{i}", offset=PAGE_BYTES * (i - 1))
             nc.gpsimd.memset(page[:], 0.0)
             pages.append(page)
 
@@ -106,13 +115,22 @@ def tile_list_outlier_features_out_kernel(tc, xq_words, xq_scales, wb_words, wb_
 
         p_tiles = []
         for i in range(TILES):
-            tok = slice(i * P, (i + 1) * P)
-            acc = banks[3 + i % 2]
-            nc.tensor.matmul_mx(out=acc[:], lhsT=xf_codes[:, tok].bitcast(FP8X4), lhsT_scale=xf_plane[:, tok],
-                                rhs=wo_codes[:].bitcast(FP8X4), rhs_scale=wo_plane[:], start=True, stop=True)
-            p_sb = late.tile([P, J], F32, name=f"p{i}", offset=4 * N * 2 if i == 0 else 4 * N * 3 + 4 * J * i)
-            nc.scalar.copy(out=p_sb[:], in_=acc[:])
-            p_tiles.append(p_sb)
+            tokens = slice(i * P, (i + 1) * P)
+            bank = banks[STAGE_BANKS[i % 2]]
+            nc.tensor.matmul_mx(
+                out=bank[:],
+                lhsT=xf_codes[:, tokens].bitcast(FP8X4),
+                lhsT_scale=xf_scale[:, tokens],
+                rhs=wo_codes[:].bitcast(FP8X4),
+                rhs_scale=wo_scale[:],
+                start=True,
+                stop=True,
+            )
+            on_page3 = PAGE_BYTES * 2
+            behind_pages = PAGE_BYTES * 3 + 4 * J * i
+            p_tile = shared.tile([P, J], F32, name=f"p{i}", offset=on_page3 if i == 0 else behind_pages)
+            nc.scalar.copy(out=p_tile[:], in_=bank[:])
+            p_tiles.append(p_tile)
 
         def scatter(i):
             nc.vector.tensor_copy(pages[i][:].indirect(offsets[:]), p_tiles[i][:])
@@ -122,60 +140,62 @@ def tile_list_outlier_features_out_kernel(tc, xq_words, xq_scales, wb_words, wb_
         for i in range(1, TILES):
             scatter(i)
 
-        nc.tensor.transpose(banks[5][:, 0:P], b_rows[:], ident[:])
-        nc.scalar.copy(out=b_cols[:], in_=banks[5][:, 0 : N // P])
+        nc.tensor.transpose(banks[SPARE_BANKS[0]][:, 0:P], b_rows[:], ident[:])
+        nc.scalar.copy(out=b_cols[:], in_=banks[SPARE_BANKS[0]][:, 0 : N // P])
 
         zb = []
 
-        def products(ks):
-            for k in ks:
-                nb = len(zb)
-                acc = banks[k]
-                nc.tensor.matmul_mx(out=acc[:], lhsT=wb_codes[:, 2 * P * nb : 2 * P * (nb + 1)].bitcast(FP4X4),
-                                    lhsT_scale=wb_plane[:, P * nb : P * (nb + 1)],
-                                    rhs=xq_codes[:].bitcast(FP4X4), rhs_scale=xq_plane[:], start=True, stop=True)
-                z_sb = keep.tile([P, T], F32, name=f"zb{nb}")
-                nc.scalar.activation(out=z_sb[:], in_=acc[:], func=IDENT, bias=b_cols[:, nb : nb + 1])
-                zb.append(z_sb)
+        def z_blocks(count):
+            for m in range(len(zb), len(zb) + count):
+                bank = banks[m % BLOCKS]
+                nc.tensor.matmul_mx(
+                    out=bank[:],
+                    lhsT=wb_codes[:, 2 * P * m : 2 * P * (m + 1)].bitcast(FP4X4),
+                    lhsT_scale=wb_scale[:, P * m : P * (m + 1)],
+                    rhs=xq_codes[:].bitcast(FP4X4),
+                    rhs_scale=xq_scale[:],
+                    start=True,
+                    stop=True,
+                )
+                block = keep.tile([P, T], F32, name=f"zb{m}")
+                nc.scalar.activation(out=block[:], in_=bank[:], func=IDENTITY, bias=b_cols[:, m : m + 1])
+                zb.append(block)
 
-        def turn(i, c, acc):
+        def turn(i, c, bank):
             for j in range(BLOCKS):
-                nc.tensor.transpose(acc[:, j * P : (j + 1) * P], zb[c * BLOCKS + j][:, i * P : (i + 1) * P], ident[:])
+                nc.tensor.transpose(bank[:, j * P : (j + 1) * P], zb[c * BLOCKS + j][:, i * P : (i + 1) * P], ident[:])
 
-        def store(i, c, res):
-            nc.sync.dma_start(out=out[i * P : (i + 1) * P, c * BANK : (c + 1) * BANK], in_=res[:])
+        def store(i, c, result):
+            nc.sync.dma_start(out=out[i * P : (i + 1) * P, c * CHUNK : (c + 1) * CHUNK], in_=result[:])
 
-        def g_unit(i, c, k):
+        def gpsimd_unit(i, c, k):
             turn(i, c, banks[k])
-            stage = keep.tile([P, BANK], F32, name=f"stage{i}_{c}")
-            nc.scalar.copy(out=stage[:], in_=banks[k][:])
-            res = keep.tile([P, BANK], F32, name=f"res{i}_{c}")
-            nc.gpsimd.tensor_tensor(res[:], stage[:], pages[i][:, c * BANK : (c + 1) * BANK], ADD)
-            store(i, c, res)
+            staged = keep.tile([P, CHUNK], F32, name=f"staged{i}_{c}")
+            nc.scalar.copy(out=staged[:], in_=banks[k][:])
+            result = keep.tile([P, CHUNK], F32, name=f"result{i}_{c}")
+            nc.gpsimd.tensor_tensor(result[:], staged[:], pages[i][:, c * CHUNK : (c + 1) * CHUNK], ADD)
+            store(i, c, result)
 
-        def v_unit(i, c, k):
+        def vector_unit(i, c, k):
             turn(i, c, banks[k])
-            res = keep.tile([P, BANK], F32, name=f"res{i}_{c}")
-            nc.vector.tensor_tensor(res[:], banks[k][:], pages[i][:, c * BANK : (c + 1) * BANK], ADD)
-            store(i, c, res)
+            result = keep.tile([P, CHUNK], F32, name=f"result{i}_{c}")
+            nc.vector.tensor_tensor(result[:], banks[k][:], pages[i][:, c * CHUNK : (c + 1) * CHUNK], ADD)
+            store(i, c, result)
 
-        products([0, 1, 2, 0])
-        g_unit(0, 0, 3)
-        g_unit(1, 0, 4)
-        products([1, 2, 0, 1])
-        g_unit(0, 1, 3)
-        g_unit(1, 1, 4)
-        products([2, 5, 6, 7, 0, 1])
-        g_unit(0, 2, 3)
-        g_unit(1, 2, 4)
-        v_unit(2, 0, 5)
-        v_unit(3, 0, 6)
-        v_unit(2, 1, 7)
-        v_unit(3, 1, 0)
-        v_unit(2, 2, 1)
-        products([2, 3])
-        g_unit(0, 3, 4)
-        v_unit(3, 2, 2)
-        v_unit(1, 3, 5)
-        v_unit(2, 3, 6)
-        v_unit(3, 3, 7)
+        last = CHUNKS - 1
+        for c in range(last - 1):
+            z_blocks(BLOCKS)
+            gpsimd_unit(0, c, STAGE_BANKS[0])
+            gpsimd_unit(1, c, STAGE_BANKS[1])
+        z_blocks(BLOCKS + BLOCKS // 2)
+        gpsimd_unit(0, last - 1, STAGE_BANKS[0])
+        gpsimd_unit(1, last - 1, STAGE_BANKS[1])
+        z_blocks(BLOCKS // 2)
+        free_order = (0, 1, STAGE_BANKS[0], STAGE_BANKS[1], 2, 3)
+        waiting = [(i, c) for c in range(last) for i in (2, 3)]
+        for (i, c), k in zip(waiting, free_order):
+            vector_unit(i, c, k)
+        gpsimd_unit(0, last, 0)
+        vector_unit(1, last, SPARE_BANKS[0])
+        vector_unit(2, last, SPARE_BANKS[1])
+        vector_unit(3, last, 1)

@@ -73,8 +73,9 @@ def tile_list_outlier_features_out_kernel(
         banks = [psum.tile([P, CHUNK], F32, name=f"bank{k}") for k in range(8)]
 
         nc.gpsimd.memset(wo_scale[:].bitcast(U32), 0)
-        nc.gpsimd.memset(xq_scale[:].bitcast(U32), 0)
+        make_identity(nc, ident[:])
         nc.gpsimd.memset(b_rows[:], 0.0)
+        nc.gpsimd.memset(xq_scale[:].bitcast(U32), 0)
         nc.vector.memset(wb_scale[:].bitcast(U32), 0)
 
         xf_rows = xf.rearrange("(p j) t -> p j t", j=PACK)
@@ -85,9 +86,8 @@ def tile_list_outlier_features_out_kernel(
         nc.sync.dma_start(out=xf_high[:], in_=xf_rows[:, :, 2 * P : T])
         nc.sync.dma_start(out=wb_codes[:].bitcast(I32), in_=wb_words[0].bitcast(I32))
         nc.sync.dma_start(out=xq_codes[:].bitcast(I32), in_=xq_words[0].bitcast(I32))
-        load_scales([nc.gpsimd, nc.gpsimd, nc.sync, nc.sync], xq_scale, xq_scales)
         nc.gpsimd.dma_start(out=b_rows[0 : N // P, :], in_=b.rearrange("o (c m) -> (o c) m", m=P))
-        make_identity(nc, ident[:])
+        load_scales([nc.gpsimd, nc.gpsimd, nc.sync, nc.sync], xq_scale, xq_scales)
         load_scales([nc.sync] * 4, wb_scale, wb_scales)
 
         pages = [keep.tile([P, N], F32, name="page0")]
@@ -165,37 +165,37 @@ def tile_list_outlier_features_out_kernel(
             for j in range(BLOCKS):
                 nc.tensor.transpose(bank[:, j * P : (j + 1) * P], zb[c * BLOCKS + j][:, i * P : (i + 1) * P], ident[:])
 
-        def store(i, c, result):
-            nc.sync.dma_start(out=out[i * P : (i + 1) * P, c * CHUNK : (c + 1) * CHUNK], in_=result[:])
+        def store(queue, i, c, result):
+            queue.dma_start(out=out[i * P : (i + 1) * P, c * CHUNK : (c + 1) * CHUNK], in_=result[:])
 
-        def gpsimd_unit(i, c, k):
+        def gpsimd_unit(i, c, k, queue):
             turn(i, c, banks[k])
             staged = keep.tile([P, CHUNK], F32, name=f"staged{i}_{c}")
             nc.scalar.copy(out=staged[:], in_=banks[k][:])
             result = keep.tile([P, CHUNK], F32, name=f"result{i}_{c}")
             nc.gpsimd.tensor_tensor(result[:], staged[:], pages[i][:, c * CHUNK : (c + 1) * CHUNK], ADD)
-            store(i, c, result)
+            store(queue, i, c, result)
 
         def vector_unit(i, c, k):
             turn(i, c, banks[k])
             result = keep.tile([P, CHUNK], F32, name=f"result{i}_{c}")
             nc.vector.tensor_tensor(result[:], banks[k][:], pages[i][:, c * CHUNK : (c + 1) * CHUNK], ADD)
-            store(i, c, result)
+            store(nc.sync, i, c, result)
 
         last = CHUNKS - 1
         for c in range(last - 1):
             z_blocks(BLOCKS)
-            gpsimd_unit(0, c, STAGE_BANKS[0])
-            gpsimd_unit(1, c, STAGE_BANKS[1])
+            gpsimd_unit(0, c, STAGE_BANKS[0], nc.sync)
+            gpsimd_unit(1, c, STAGE_BANKS[1], nc.sync)
         z_blocks(BLOCKS + BLOCKS // 2)
-        gpsimd_unit(0, last - 1, STAGE_BANKS[0])
-        gpsimd_unit(1, last - 1, STAGE_BANKS[1])
+        gpsimd_unit(0, last - 1, STAGE_BANKS[0], nc.sync)
+        gpsimd_unit(1, last - 1, STAGE_BANKS[1], nc.sync)
         z_blocks(BLOCKS // 2)
         free_order = (0, 1, STAGE_BANKS[0], STAGE_BANKS[1], 2, 3)
         waiting = [(i, c) for c in range(last) for i in (2, 3)]
         for (i, c), k in zip(waiting, free_order):
             vector_unit(i, c, k)
-        gpsimd_unit(0, last, 0)
+        gpsimd_unit(0, last, 0, nc.scalar)
         vector_unit(1, last, SPARE_BANKS[0])
         vector_unit(2, last, SPARE_BANKS[1])
         vector_unit(3, last, 1)

from contextlib import ExitStack

import concourse.mybir as mybir
from concourse.masks import make_identity

K, T, N, J = 512, 512, 2048, 512
FLOPS = 2 * K * T * N + 2 * K * T * J

F32 = mybir.dt.float32
BF16 = mybir.dt.bfloat16
I32 = mybir.dt.int32
U32 = mybir.dt.uint32
U16 = mybir.dt.uint16
U8 = mybir.dt.uint8
FP8X4 = mybir.dt.float8_e4m3fn_x4
FP4X4 = mybir.dt.float4_e2m1fn_x4
ADD = mybir.AluOpType.add
IDENTITY = mybir.ActivationFunctionType.Identity

P = 128
PACK = 4
CHUNK = 512
TILES = T // P
CHUNKS = N // CHUNK
BLOCKS = CHUNK // P
PAGE_BYTES = 4 * N
RUN = 4

STAGE_BANKS = (4, 5)
SPARE_BANKS = (6, 7)


def load_scales(queues, scale_tile, scales):
    rows = scales[0].bitcast(I32).rearrange("(q r) n -> r q n", r=4)
    dst = scale_tile[:].bitcast(I32)
    for r in range(4):
        queues[r].dma_start(out=dst[r:P:32, :], in_=rows[r])


def interleave(nc, grouped, raw):
    nc.vector.tensor_copy(
        out=grouped.rearrange("p (c i j) -> p c j i", i=RUN, j=PACK),
        in_=raw.rearrange("p j (c i) -> p c j i", i=RUN),
    )


def tile_list_outlier_features_out_kernel(
    tc, xq_words, xq_scales, wb_words, wb_scales, xf, wo_words, wo_scales, b, offs, out
):
    nc = tc.nc
    with ExitStack() as ctx:
        keep = ctx.enter_context(tc.tile_pool(name="keep", bufs=1))
        shared = ctx.enter_context(tc.tile_pool(name="shared", bufs=1))
        psum = ctx.enter_context(tc.psum_pool(name="psum", bufs=1))

        offsets = keep.tile([P, J // 16], U16, name="offsets")
        ident = keep.tile([P, P], F32, name="ident")
        wo_scale = keep.tile([P, J], U8, name="wo_scale", align_bytes=64)
        xq_scale = keep.tile([P, T], U8, name="xq_scale", align_bytes=64)
        wb_scale = keep.tile([P, N], U8, name="wb_scale", align_bytes=64)
        wo_codes = keep.tile([P, J], U32, name="wo_codes", align_bytes=64)
        xq_codes = keep.tile([P, 2 * T], U8, name="xq_codes", align_bytes=64)
        wb_codes = keep.tile([P, 2 * N], U8, name="wb_codes", align_bytes=64)
        xf_low = keep.tile([P, PACK, 2 * P], F32, name="xf_low")
        xf_high = keep.tile([P, PACK, 2 * P], F32, name="xf_high")
        grouped0 = keep.tile([P, PACK * P], BF16, name="grouped0", align_bytes=64)
        grouped1 = keep.tile([P, PACK * P], BF16, name="grouped1", align_bytes=64)
        grouped23 = shared.tile([P, 2 * PACK * P], BF16, name="grouped23", align_bytes=64, offset=PAGE_BYTES - 1024)
        xf_codes = keep.tile([P, T], U32, name="xf_codes", align_bytes=64)
        xf_scale = keep.tile([P, T], U8, name="xf_scale", align_bytes=64)
        b_rows = keep.tile([P, P], F32, name="b_rows")
        b_cols = keep.tile([P, N // P], F32, name="b_cols")
        banks = [psum.tile([P, CHUNK], F32, name=f"bank{k}") for k in range(8)]

        nc.gpsimd.memset(wo_scale[:].bitcast(U32), 0)
        make_identity(nc, ident[:])
        nc.gpsimd.memset(b_rows[:], 0.0)
        nc.gpsimd.memset(xq_scale[:].bitcast(U32), 0)
        nc.vector.memset(wb_scale[:].bitcast(U32), 0)

        xf_rows = xf.rearrange("(p j) t -> p j t", j=PACK)
        nc.sync.dma_start(offsets[:], offs)
        nc.sync.dma_start(out=xf_low[:], in_=xf_rows[:, :, 0 : 2 * P])
        nc.sync.dma_start(out=wo_codes[:].bitcast(I32), in_=wo_words[0].rearrange("p n t -> p (n t)").bitcast(I32))
        load_scales([nc.sync] * 4, wo_scale, wo_scales)
        nc.sync.dma_start(out=xf_high[:], in_=xf_rows[:, :, 2 * P : T])
        nc.sync.dma_start(out=wb_codes[:].bitcast(I32), in_=wb_words[0].bitcast(I32))
        nc.sync.dma_start(out=xq_codes[:].bitcast(I32), in_=xq_words[0].bitcast(I32))
        nc.gpsimd.dma_start(out=b_rows[0 : N // P, :], in_=b.rearrange("o (c m) -> (o c) m", m=P))
        load_scales([nc.gpsimd, nc.gpsimd, nc.sync, nc.sync], xq_scale, xq_scales)
        load_scales([nc.sync] * 4, wb_scale, wb_scales)

        pages = [keep.tile([P, N], F32, name="page0")]
        nc.vector.memset(pages[0][:].bitcast(U32), 0)

        def quantize(grouped, first, last):
            nc.vector.quantize_mx(
                out=xf_codes[:, first:last].bitcast(FP8X4), scales=xf_scale[:, first:last], in_=grouped[:]
            )

        interleave(nc, grouped0[:], xf_low[:, :, 0:P])
        interleave(nc, grouped1[:], xf_low[:, :, P : 2 * P])
        quantize(grouped0, 0, P)
        quantize(grouped1, P, 2 * P)
        interleave(nc, grouped23[:], xf_high[:])
        quantize(grouped23, 2 * P, T)

        def clear_page(i):
            page = shared.tile([P, N], F32, name=f"page{i}", offset=PAGE_BYTES * (i - 1))
            nc.gpsimd.memset(page[:], 0.0)
            pages.append(page)

        clear_page(1)
        clear_page(2)

        p_tiles = []
        for i in range(TILES):
            tokens = slice(i * P, (i + 1) * P)
            bank = banks[STAGE_BANKS[i % 2]]
            nc.tensor.matmul_mx(
                out=bank[:],
                lhsT=xf_codes[:, tokens].bitcast(FP8X4),
                lhsT_scale=xf_scale[:, tokens],
                rhs=wo_codes[:].bitcast(FP8X4),
                rhs_scale=wo_scale[:],
                start=True,
                stop=True,
            )
            on_page3 = PAGE_BYTES * 2
            behind_pages = PAGE_BYTES * 3 + 4 * J * i
            p_tile = shared.tile([P, J], F32, name=f"p{i}", offset=on_page3 if i == 0 else behind_pages)
            nc.scalar.copy(out=p_tile[:], in_=bank[:])
            p_tiles.append(p_tile)

        def scatter(i):
            nc.vector.tensor_copy(pages[i][:].indirect(offsets[:]), p_tiles[i][:])

        scatter(0)
        clear_page(3)
        for i in range(1, TILES):
            scatter(i)

        nc.tensor.transpose(banks[SPARE_BANKS[0]][:, 0:P], b_rows[:], ident[:])
        nc.scalar.copy(out=b_cols[:], in_=banks[SPARE_BANKS[0]][:, 0 : N // P])

        zb = []

        def z_blocks(count):
            for m in range(len(zb), len(zb) + count):
                bank = banks[m % BLOCKS]
                nc.tensor.matmul_mx(
                    out=bank[:],
                    lhsT=wb_codes[:, 2 * P * m : 2 * P * (m + 1)].bitcast(FP4X4),
                    lhsT_scale=wb_scale[:, P * m : P * (m + 1)],
                    rhs=xq_codes[:].bitcast(FP4X4),
                    rhs_scale=xq_scale[:],
                    start=True,
                    stop=True,
                )
                block = keep.tile([P, T], F32, name=f"zb{m}")
                nc.scalar.activation(out=block[:], in_=bank[:], func=IDENTITY, bias=b_cols[:, m : m + 1])
                zb.append(block)

        def turn(i, c, bank):
            for j in range(BLOCKS):
                nc.tensor.transpose(bank[:, j * P : (j + 1) * P], zb[c * BLOCKS + j][:, i * P : (i + 1) * P], ident[:])

        def store(queue, i, c, result):
            queue.dma_start(out=out[i * P : (i + 1) * P, c * CHUNK : (c + 1) * CHUNK], in_=result[:])

        def gpsimd_unit(i, c, k, queue):
            turn(i, c, banks[k])
            staged = keep.tile([P, CHUNK], F32, name=f"staged{i}_{c}")
            nc.scalar.copy(out=staged[:], in_=banks[k][:])
            result = keep.tile([P, CHUNK], F32, name=f"result{i}_{c}")
            nc.gpsimd.tensor_tensor(result[:], staged[:], pages[i][:, c * CHUNK : (c + 1) * CHUNK], ADD)
            store(queue, i, c, result)

        def vector_unit(i, c, k):
            turn(i, c, banks[k])
            result = keep.tile([P, CHUNK], F32, name=f"result{i}_{c}")
            nc.vector.tensor_tensor(result[:], banks[k][:], pages[i][:, c * CHUNK : (c + 1) * CHUNK], ADD)
            store(nc.sync, i, c, result)

        last = CHUNKS - 1
        for c in range(last - 1):
            z_blocks(BLOCKS)
            gpsimd_unit(0, c, STAGE_BANKS[0], nc.sync)
            gpsimd_unit(1, c, STAGE_BANKS[1], nc.sync)
        z_blocks(BLOCKS + BLOCKS // 2)
        gpsimd_unit(0, last - 1, STAGE_BANKS[0], nc.sync)
        gpsimd_unit(1, last - 1, STAGE_BANKS[1], nc.sync)
        z_blocks(BLOCKS // 2)
        free_order = (0, 1, STAGE_BANKS[0], STAGE_BANKS[1], 2, 3)
        waiting = [(i, c) for c in range(last) for i in (2, 3)]
        for (i, c), k in zip(waiting, free_order):
            vector_unit(i, c, k)
        gpsimd_unit(0, last, 0, nc.scalar)
        vector_unit(1, last, SPARE_BANKS[0])
        vector_unit(2, last, SPARE_BANKS[1])
        vector_unit(3, last, 1)
